import numpy as np
import ml_dtypes


def mxq(x, axis, fmt="e4m3"):
    dtype, down = {"e4m3": (ml_dtypes.float8_e4m3fn, 7), "e5m2": (ml_dtypes.float8_e5m2, 14)}[fmt]
    v = np.moveaxis(np.asarray(x, np.float32).astype(ml_dtypes.bfloat16).astype(np.float64), axis, -1)
    blocks = v.reshape(v.shape[:-1] + (-1, 32))
    amax = np.abs(blocks).max(-1, keepdims=True)
    byte = np.maximum(np.where(amax > 0, np.frexp(amax)[1] - 1 + 127, 0) - down, 1)
    scale = np.exp2(byte - 127.0)
    codes = (blocks / scale).astype(np.float32).astype(dtype).astype(np.float64)
    return np.moveaxis((codes * scale).reshape(v.shape), -1, axis)


WIDE = False


def mx_kscale(k):
    if not WIDE:
        return np.ones(k)
    levels = np.array([10, -10, 5, -5, 0])
    if k % 512:
        return np.exp2(np.random.permutation(np.resize(levels, k // 32))).repeat(32)
    a = np.empty((k // 512, 16))
    for p in range(k // 512):
        a[p, :8] = np.random.permutation(np.resize(levels, 8))
        for g in range(8):
            far = levels[np.abs(levels - a[p, g]) >= 10]
            a[p, g + 8] = far[np.random.randint(len(far))]
    return np.exp2(a.ravel()).repeat(32)


BF16 = ml_dtypes.bfloat16


def bf(x):
    return np.asarray(x, np.float32).astype(BF16)


def f64(x):
    return np.asarray(x).astype(np.float64)


NQ, ND, D = 1024, 1536, 1024


def row_softmax(x):
    e = np.exp(x - np.max(x, axis=1, keepdims=True))
    return e / np.sum(e, axis=1, keepdims=True)


def draw0():
    s, t, u = mx_kscale(D), mx_kscale(ND), mx_kscale(NQ)
    return {
        "q": bf(np.random.standard_normal((NQ, D)) * s[None, :]),
        "d": bf(np.random.standard_normal((ND, D)) / s[None, :]),
        "teacher": bf(np.random.standard_normal((NQ, ND))),
        "dr": bf(np.random.standard_normal((ND, D)) / np.sqrt(ND) / t[:, None]),
        "qr": bf(np.random.standard_normal((NQ, D)) / np.sqrt(NQ) / u[:, None]),
        "wd": bf((1.0 + 0.1 * np.random.standard_normal(ND)) * t),
        "wq": bf((1.0 + 0.1 * np.random.standard_normal(NQ)) * u),
    }


def core(q, d, teacher, dr, qr, wd, wq):
    n_docs = d.shape[0]
    scale = 1.0 / np.sqrt(q.shape[1])

    s = scale * (mxq(f64(q), 1, "e4m3") @ mxq(f64(d), 1, "e4m3").T)

    p = row_softmax(s)
    t = row_softmax(f64(teacher))

    g = float(n_docs) * (p - t)

    gd = g * f64(wd)[None, :]
    dq = mxq(gd, 1, "e4m3") @ mxq(f64(dr), 0, "e4m3")

    gq = g * f64(wq)[:, None]
    dd = mxq(gq, 0, "e4m3").T @ mxq(f64(qr), 0, "e4m3")

    return dq, dd


def e4m3fn_bytes(y):
    return np.clip(np.asarray(y, np.float64), -448.0, 448.0).astype(np.float32).astype(ml_dtypes.float8_e4m3fn).view(np.uint8)


def e4m3fn_values(b):
    return np.asarray(b, np.uint8).view(ml_dtypes.float8_e4m3fn).astype(np.float64)


def setup_inputs():
    d = draw0()
    x0 = np.asarray(d['dr']).astype(np.float64)
    s = (np.max(np.abs(x0), axis=(1,), keepdims=True) / 448.0).astype(np.float32)
    out = {}
    for k, v in d.items():
        if k == 'dr':
            out['dr_bytes'] = e4m3fn_bytes(x0 / s.astype(np.float64))
            out['dr_scale'] = s
        else:
            out[k] = v
    return out


def reference(q, d, teacher, dr_bytes, dr_scale, qr, wd, wq):
    return core(q, d, teacher, e4m3fn_values(dr_bytes) * dr_scale.astype(np.float64), qr, wd, wq)

@@ -1,0 +1,494 @@
+from contextlib import ExitStack
+
+import concourse.mybir as mybir
+from concourse.masks import make_identity
+
+NQ, ND, D = 1024, 1536, 1024
+FLOPS = 3 * 2 * NQ * ND * D
+
+F32 = mybir.dt.float32
+BF16 = mybir.dt.bfloat16
+U32 = mybir.dt.uint32
+U8 = mybir.dt.uint8
+FP8 = mybir.dt.float8_e4m3fn
+FP8X4 = mybir.dt.float8_e4m3fn_x4
+ALU = mybir.AluOpType
+ACT = mybir.ActivationFunctionType
+
+P = 128
+PACK = 4
+GROUPS = 2
+TILES = 8
+SCALE = 1.0 / 32.0
+
+
+def tile_crossencoderdistillbiencodergrad_kernel(
+    tc, q, d, teacher, dr_bytes, dr_scale, qr, wd, wq, out_0, out_1
+):
+    nc = tc.nc
+
+    q_v = q.rearrange("(g p t) k -> g p t k", p=P, t=PACK)
+    d_v = d.rearrange("(r p) k -> p r k", p=P)
+    te_v = teacher.rearrange("(g p t) n -> g p t n", p=P, t=PACK)
+    drb_v = dr_bytes.rearrange("(s p t) n -> s p t n", p=P, t=PACK)
+    drs_v = dr_scale.rearrange("(s p t) o -> p s (t o)", p=P, t=PACK)
+    qr_v = qr.rearrange("(g p t) n -> g p t n", p=P, t=PACK)
+    wq_v = wq.rearrange("(g p t) -> p g t", p=P, t=PACK)
+    dq_v = out_0.rearrange("(g p t) n -> g t p n", p=P, t=PACK)
+    dd_v = out_1.rearrange("(j p) n -> j p n", p=P)
+
+    with ExitStack() as ctx:
+        keep = ctx.enter_context(tc.tile_pool(name="keep", bufs=1))
+        pool = ctx.enter_context(tc.tile_pool(name="work", bufs=1))
+        psum = ctx.enter_context(tc.psum_pool(name="psum", bufs=1))
+
+        ident = keep.tile([P, P], F32, name="ident")
+        q_codes = keep.tile([P, TILES, 2, P], U32, name="q_codes", align_bytes=64)
+        q_scales = keep.tile([P, TILES, 2, P], U8, name="q_scales", align_bytes=64)
+        d_codes = keep.tile([P, 2, ND], U32, name="d_codes", align_bytes=64)
+        d_scales = keep.tile([P, 2, ND], U8, name="d_scales", align_bytes=64)
+        dr_codes = keep.tile([P, 3, D], U32, name="dr_codes", align_bytes=64)
+        dr_scales = keep.tile([P, 3, D], U8, name="dr_scales", align_bytes=64)
+        qr_codes = keep.tile([P, 2, D], U32, name="qr_codes", align_bytes=64)
+        qr_scales = keep.tile([P, 2, D], U8, name="qr_scales", align_bytes=64)
+        gq_codes = keep.tile([P, 2, ND], U32, name="gq_codes", align_bytes=64)
+        gq_scales = keep.tile([P, 2, ND], U8, name="gq_scales", align_bytes=64)
+
+        drs = keep.tile([P, 3, PACK], F32, name="drs")
+        wq_raw = keep.tile([P, GROUPS, PACK], BF16, name="wq_raw")
+        wq_big = keep.tile([P, TILES], F32, name="wq_big")
+        wd_big = keep.tile([P, ND], F32, name="wd_big")
+        cwq = keep.tile([P, TILES], F32, name="cwq")
+        s_min = keep.tile([P, TILES, 4], F32, name="s_min")
+        s_neg = keep.tile([P, TILES], F32, name="s_neg")
+        t_neg = keep.tile([P, TILES], F32, name="t_neg")
+        s_sum = keep.tile([P, TILES], F32, name="s_sum")
+        t_sum = keep.tile([P, TILES], F32, name="t_sum")
+        t_rec = keep.tile([P, TILES], F32, name="t_rec")
+        s_rec = keep.tile([P, TILES], F32, name="s_rec")
+        ratio = keep.tile([P, TILES], F32, name="ratio")
+        dummy = keep.tile([P, 2], F32, name="dummy")
+
+        q_raw, dr_raw, te_raw, qr_raw = {}, {}, {}, {}
+        d_raw = pool.tile([P, 12, D], BF16, name="d_raw", tag="big", bufs=2)
+        wd_raw = pool.tile([P, ND], BF16, name="wd_raw", tag="gd", bufs=2)
+
+        def load_te(i):
+            te_raw[i] = pool.tile([P, ND], BF16, name="te_raw", tag="te", bufs=5)
+            nc.sync.dma_start(out=te_raw[i][:], in_=te_v[i // PACK, :, i % PACK, :])
+
+        def load_dr(s):
+            dr_raw[s] = pool.tile([P, PACK, D], U8, name="dr_raw", tag="drb", bufs=2)
+            nc.sync.dma_start(out=dr_raw[s][:], in_=drb_v[s])
+
+        def load_d(r, n):
+            nc.sync.dma_start(out=d_raw[:, r : r + n, :], in_=d_v[:, r : r + n, :])
+
+        def load_qr(g):
+            qr_raw[g] = pool.tile([P, PACK, D], BF16, name="qr_raw", tag="q8", bufs=3)
+            nc.sync.dma_start(out=qr_raw[g][:], in_=qr_v[g])
+
+        for g in range(GROUPS):
+            q_raw[g] = pool.tile([P, PACK, D], BF16, name="q_raw", tag="q8", bufs=3)
+        load_te(0)
+        nc.scalar.dma_start(out=drs[:], in_=drs_v)
+        load_dr(0)
+        nc.sync.dma_start(out=q_raw[0][:, 0, :], in_=q_v[0, :, 0, :])
+        for r in range(0, 4, 2):
+            load_d(r, 2)
+        load_te(1)
+        for r in range(4, 12, 2):
+            load_d(r, 2)
+        nc.sync.dma_start(out=q_raw[0][:, 1:4, :], in_=q_v[0, :, 1:4, :])
+        nc.sync.dma_start(out=wq_raw[:], in_=wq_v)
+        nc.sync.dma_start(out=wd_raw[:], in_=wd.partition_broadcast(P))
+        load_dr(1)
+        load_te(2)
+        nc.sync.dma_start(out=q_raw[1][:], in_=q_v[1])
+        load_te(3)
+        load_te(4)
+        load_qr(0)
+
+        nc.gpsimd.memset(dummy[:], 0.0)
+        nc.scalar.activation(out=dummy[:, 1:2], in_=dummy[:, 0:1], func=ACT.Exp)
+        make_identity(nc, ident[:])
+
+        def quantize(codes, scales, grouped):
+            nc.vector.quantize_mx(out=codes.bitcast(FP8X4), scales=scales, in_=grouped)
+
+        banks = (("tp", 2), ("o", 3), ("s", 3))
+        count = [0]
+
+        def transpose_bank():
+            tag, bufs = banks[count[0] % 3]
+            count[0] += 1
+            return psum.tile([P, 2, 2, P], F32, name="tbank", tag=tag, bufs=bufs)
+
+        def copy_out(eng, out, in_):
+            if eng == "V":
+                nc.vector.tensor_copy(out=out, in_=in_)
+            else:
+                nc.scalar.copy(out=out, in_=in_)
+
+        def as_words(grp):
+            return grp[:].rearrange("p c e -> p (c e)").bitcast(F32)
+
+        sb = {}
+        later = []
+
+        def prep_d(rr):
+            for s in range(2):
+                bank = transpose_bank()
+                for j in range(2):
+                    words = d_raw[:, 2 * rr + j, :].bitcast(F32)
+                    for u in range(2):
+                        nc.tensor.transpose(bank[:, j, u, :], words[:, 256 * s + u : 256 * (s + 1) : 2], ident[:])
+                sb["d", rr, s] = bank
+
+        def d_out(rr, engines):
+            for s in range(2):
+                grp = pool.tile([P, 256, PACK], BF16, name="agrp", tag="agrp", bufs=4, align_bytes=64)
+                copy_out(
+                    engines[s], as_words(grp).rearrange("p (j c u) -> p j c u", j=2, u=2),
+                    sb["d", rr, s][:].rearrange("p j u c -> p j c u"),
+                )
+                cols = slice(256 * rr, 256 * (rr + 1))
+                later.append((d_codes[:, s, cols], d_scales[:, s, cols], grp[:].rearrange("p c e -> p (c e)")))
+
+        def flush(n=99):
+            for k in range(min(n, len(later))):
+                quantize(*later.pop(0))
+
+        def prep_q(i, eng):
+            q_turn(i)
+            q_out(i, eng)
+
+        def q_turn(i):
+            words = q_raw[i // PACK][:, i % PACK, :].bitcast(F32)
+            bank = transpose_bank() if i == 0 else psum.tile([P, 2, 2, P], F32, name="tbank", tag="tp", bufs=2)
+            for s in range(2):
+                for u in range(2):
+                    nc.tensor.transpose(bank[:, s, u, :], words[:, 256 * s + u : 256 * (s + 1) : 2], ident[:])
+            sb["q", i] = bank
+
+        def q_out(i, eng):
+            bank = sb["q", i]
+            grp = pool.tile([P, 256, PACK], BF16, name="agrp", tag="agrp", bufs=4, align_bytes=64)
+            copy_out(
+                eng, as_words(grp).rearrange("p (j c u) -> p j c u", j=2, u=2),
+                bank[:].rearrange("p j u c -> p j c u"),
+            )
+            later.append((
+                q_codes[:, i].rearrange("p s c -> p (s c)"), q_scales[:, i].rearrange("p s c -> p (s c)"),
+                grp[:].rearrange("p c e -> p (c e)"),
+            ))
+
+        wides = {}
+
+        def widen(s, h, engines="SSSS"):
+            cols = slice(512 * h, 512 * (h + 1))
+            wide = pool.tile([P, PACK, 512], BF16, name="wide", tag="wide", bufs=2, align_bytes=64)
+            for t in range(PACK):
+                if engines[t] == "S":
+                    nc.scalar.activation(
+                        out=wide[:, t, :], in_=dr_raw[s][:, t, cols].bitcast(FP8), func=ACT.Copy,
+                        scale=drs[:, s, t : t + 1],
+                    )
+                else:
+                    nc.vector.tensor_scalar(
+                        out=wide[:, t, :], in0=dr_raw[s][:, t, cols].bitcast(FP8), scalar1=drs[:, s, t : t + 1],
+                        scalar2=None, op0=ALU.mult,
+                    )
+            wides[s, h] = wide
+
+        def lace(s, h, eng="V"):
+            cols = slice(512 * h, 512 * (h + 1))
+            grp = pool.tile([P, 512, PACK], BF16, name="rgrp", tag="rgrp", bufs=2, align_bytes=64)
+            copy_out(
+                eng, grp[:].rearrange("p (c i) t -> p c t i", i=4),
+                wides.pop((s, h))[:].rearrange("p t (c i) -> p c t i", i=4),
+            )
+            later.append((dr_codes[:, s, cols], dr_scales[:, s, cols], grp[:].rearrange("p c t -> p (c t)")))
+
+        def lace_qr(g, h, eng="S"):
+            cols = slice(512 * h, 512 * (h + 1))
+            grp = pool.tile([P, 512, PACK], BF16, name="rgrp", tag="rgrp", bufs=2, align_bytes=64)
+            copy_out(
+                eng, grp[:].rearrange("p (c i) t -> p c t i", i=4),
+                qr_raw[g][:, :, cols].rearrange("p t (c i) -> p c t i", i=4),
+            )
+            later.append((qr_codes[:, g, cols], qr_scales[:, g, cols], grp[:].rearrange("p c t -> p (c t)")))
+
+        te_exp, es, gds, gd_grp, gdT, obanks = {}, {}, {}, {}, {}, {}
+
+        def te_max(i):
+            nc.vector.tensor_scalar(
+                out=te_raw[i][:], in0=te_raw[i][:], scalar1=-1.0, scalar2=None, op0=ALU.mult, op1=ALU.min,
+                accum_out=t_neg[:, i : i + 1],
+            )
+
+        def te_e(i):
+            te_exp[i] = pool.tile([P, ND], F32, name="te_exp", tag="te_exp", bufs=2)
+            nc.scalar.activation(
+                out=te_exp[i][:], in_=te_raw[i][:], func=ACT.Exp, scale=-1.0, bias=t_neg[:, i : i + 1],
+                accum_out=t_sum[:, i : i + 1],
+            )
+
+        def scores(i, chunks=(0, 1, 2)):
+            for n in chunks:
+                cols = slice(512 * n, 512 * (n + 1))
+                sb[i, n] = psum.tile([P, 512], F32, name="sbank", tag="s", bufs=3)
+                for s in range(2):
+                    nc.tensor.matmul_mx(
+                        out=sb[i, n][:],
+                        lhsT=q_codes[:, i, s, :].bitcast(FP8X4), lhsT_scale=q_scales[:, i, s, :],
+                        rhs=d_codes[:, s, cols].bitcast(FP8X4), rhs_scale=d_scales[:, s, cols],
+                        start=(s == 0), stop=(s == 1),
+                    )
+
+        def s_max(i, chunks=(0, 1, 2)):
+            g, t = i // PACK, i % PACK
+            if g not in es:
+                es[g] = pool.tile([P, PACK, ND], F32, name="es", tag="big", bufs=2)
+            for n in chunks:
+                cols = slice(512 * n, 512 * (n + 1))
+                nc.vector.tensor_scalar(
+                    out=es[g][:, t, cols], in0=sb[i, n][:], scalar1=-SCALE, scalar2=None, op0=ALU.mult, op1=ALU.min,
+                    accum_out=s_min[:, i, n : n + 1],
+                )
+            if 2 not in chunks:
+                return
+            nc.vector.tensor_reduce(
+                out=s_neg[:, i : i + 1], in_=s_min[:, i, 0:3], op=ALU.min, axis=mybir.AxisListType.X
+            )
+
+        def s_e(i):
+            e = es[i // PACK][:, i % PACK, :]
+            nc.scalar.activation(
+                out=e, in_=e, func=ACT.Exp, scale=-1.0, bias=s_neg[:, i : i + 1], accum_out=s_sum[:, i : i + 1]
+            )
+
+        def stats(i):
+            nc.vector.reciprocal(out=t_rec[:, i : i + 1], in_=t_sum[:, i : i + 1])
+            nc.vector.reciprocal(out=s_rec[:, i : i + 1], in_=s_sum[:, i : i + 1])
+            nc.vector.tensor_scalar(
+                out=ratio[:, i : i + 1], in0=s_sum[:, i : i + 1], scalar1=t_rec[:, i : i + 1], scalar2=-1.0,
+                op0=ALU.mult, op1=ALU.mult,
+            )
+            nc.gpsimd.tensor_tensor(
+                out=cwq[:, i : i + 1], in0=s_rec[:, i : i + 1], in1=wq_big[:, i : i + 1], op=ALU.mult
+            )
+
+        def h_make(i):
+            h = es[i // PACK][:, i % PACK, :]
+            nc.vector.scalar_tensor_tensor(
+                out=h, in0=te_exp[i][:], scalar=ratio[:, i : i + 1], in1=h, op0=ALU.mult, op1=ALU.add
+            )
+
+        def gd_make(i):
+            gds[i] = pool.tile([P, ND], BF16, name="gd", tag="gd", bufs=2)
+            nc.vector.scalar_tensor_tensor(
+                out=gds[i][:], in0=es[i // PACK][:, i % PACK, :], scalar=s_rec[:, i : i + 1], in1=wd_big[:],
+                op0=ALU.mult, op1=ALU.mult,
+            )
+
+        def gd_turn(i):
+            words = gds[i][:].bitcast(F32)
+            for k, n in ((0, 2), (2, 1)):
+                bank = psum.tile([P, 2, 2, P], F32, name="gbank", tag="tp", bufs=2)
+                for s in range(k, k + n):
+                    for u in range(2):
+                        nc.tensor.transpose(bank[:, s - k, u, :], words[:, 256 * s + u : 256 * (s + 1) : 2], ident[:])
+                sb[i, "g", k] = bank
+
+        def gd_out(i, engines="SS"):
+            gd_grp[i] = pool.tile([P, 3 * P, PACK], BF16, name="gdgrp", tag="gdgrp", bufs=2, align_bytes=64)
+            grp_w = as_words(gd_grp[i]).rearrange("p (s c u) -> p s c u", s=3, u=2)
+            for e, (k, n) in zip(engines, ((0, 2), (2, 1))):
+                copy_out(e, grp_w[:, k : k + n], sb[i, "g", k][:, 0:n].rearrange("p s u c -> p s c u"))
+
+        def gd_q(i):
+            codes = pool.tile([P, 3 * P], U32, name="gdc", tag="gdc", bufs=2, align_bytes=64)
+            scales = pool.tile([P, 3 * P], U8, name="gds", tag="gds", bufs=2, align_bytes=64)
+            flat = gd_grp[i][:].rearrange("p c e -> p (c e)")
+            quantize(codes[:, 0:256], scales[:, 0:256], flat[:, 0:1024])
+            quantize(codes[:, 256:384], scales[:, 256:384], flat[:, 1024:1536])
+            gdT[i] = (codes, scales)
+
+        def dq(i):
+            codes, scales = gdT[i]
+            for h in range(2):
+                cols = slice(512 * h, 512 * (h + 1))
+                obanks[i, h] = psum.tile([P, 512], F32, name="obank", tag="o", bufs=3)
+                for s in range(3):
+                    k = slice(P * s, P * (s + 1))
+                    nc.tensor.matmul_mx(
+                        out=obanks[i, h][:],
+                        lhsT=codes[:, k].bitcast(FP8X4), lhsT_scale=scales[:, k],
+                        rhs=dr_codes[:, s, cols].bitcast(FP8X4), rhs_scale=dr_scales[:, s, cols],
+                        start=(s == 0), stop=(s == 2),
+                    )
+
+        def dq_out(i, engines="SS"):
+            res = pool.tile([P, D], F32, name="res", tag="res", bufs=3)
+            for h in range(2):
+                copy_out(engines[h], res[:, 512 * h : 512 * (h + 1)], obanks[i, h][:])
+            nc.sync.dma_start(out=dq_v[i // PACK, i % PACK], in_=res[:])
+
+        def gq(g, a, n):
+            cols = slice(128 * a, 128 * (a + n))
+            grp = pool.tile([P, 256, PACK], BF16, name="qgrp", tag="agrp", bufs=4, align_bytes=64)
+            gain = cwq[:, PACK * g : PACK * (g + 1)].unsqueeze(1).unsqueeze(3).to_broadcast([P, 32 * n, PACK, 4])
+            nc.vector.tensor_tensor(
+                out=grp[:, 0 : 128 * n].rearrange("p (c i) t -> p c t i", i=4),
+                in0=es[g][:, :, cols].rearrange("p t (c i) -> p c t i", i=4),
+                in1=gain, op=ALU.mult,
+            )
+            later.append((gq_codes[:, g, cols], gq_scales[:, g, cols], grp[:, 0 : 128 * n].rearrange("p c t -> p (c t)")))
+
+        dd_banks = (("o", 3), ("s", 3), ("tp", 2))
+        dd_count = [0]
+
+        def dd_pe(j):
+            k = slice(P * j, P * (j + 1))
+            for h in range(2):
+                cols = slice(512 * h, 512 * (h + 1))
+                tag, bufs = dd_banks[dd_count[0] % 3]
+                dd_count[0] += 1
+                bank = psum.tile([P, 512], F32, name="dbank", tag=tag, bufs=bufs)
+                for g in range(GROUPS):
+                    nc.tensor.matmul_mx(
+                        out=bank[:],
+                        lhsT=gq_codes[:, g, k].bitcast(FP8X4), lhsT_scale=gq_scales[:, g, k],
+                        rhs=qr_codes[:, g, cols].bitcast(FP8X4), rhs_scale=qr_scales[:, g, cols],
+                        start=(g == 0), stop=(g == 1),
+                    )
+                obanks["d", j, h] = bank
+
+        def dd_out(j, engines):
+            if j % 5 < 3:
+                res = pool.tile([P, D], F32, name="res", tag="res", bufs=3)
+            else:
+                res = pool.tile([P, D], F32, name="res2", tag="te_exp", bufs=2)
+            for h in range(2):
+                copy_out(engines[h], res[:, 512 * h : 512 * (h + 1)], obanks["d", j, h][:])
+            nc.sync.dma_start(out=dd_v[j], in_=res[:])
+
+        te_max(0)
+        te_e(0)
+        q_turn(0)
+        q_out(0, "S")
+        prep_d(0)
+        d_out(0, "SS")
+        widen(0, 0, "SSVV")
+        flush()
+        prep_d(1)
+        lace(0, 0, "VV"[0])
+        d_out(1, "SS")
+        widen(0, 1, "SSSV")
+        flush(1)
+        prep_d(2)
+        flush(2)
+        scores(0, (0,))
+        d_out(2, "SS")
+        lace(0, 1, "VV"[1])
+        load_dr(2)
+        prep_d(3)
+        s_max(0, (0,))
+        flush()
+        d_out(3, "SS")
+        prep_d(4)
+        te_max(1)
+        flush()
+        scores(0, (1,))
+        d_out(4, "SS")
+        prep_d(5)
+        s_max(0, (1,))
+        q_turn(1)
+        flush()
+        nc.gpsimd.tensor_scalar(
+            out=wq_big[:], in0=wq_raw[:].rearrange("p g t -> p (g t)"), scalar1=float(ND), scalar2=0.0,
+            op0=ALU.mult, op1=ALU.add,
+        )
+        nc.gpsimd.tensor_scalar(
+            out=wd_big[:], in0=wd_raw[:], scalar1=float(ND), scalar2=0.0, op0=ALU.mult, op1=ALU.add
+        )
+        d_out(5, "SV")
+        q_out(1, "S")
+        flush()
+        scores(0, (2,))
+        scores(1)
+        q_turn(2)
+        s_max(0, (2,))
+        s_e(0)
+        q_out(2, "S")
+        for h in range(2):
+            widen(1, h, "SSSS")
+            lace(1, h, "SS"[h])
+        for i in range(TILES):
+            if i == 0:
+                s_max(1, (0,))
+            stats(i)
+            if i + 3 < TILES:
+                q_turn(i + 3)
+            h_make(i)
+            if i + 1 < TILES:
+                te_e(i + 1)
+            if i + 3 < TILES:
+                q_out(i + 3, "S")
+            if i >= 1:
+                gd_q(i - 1)
+                dq(i - 1)
+            if i < 1:
+                widen(2, 0, "SSSS")
+            if i + 1 < TILES:
+                s_max(i + 1, (1, 2) if i == 0 else (0, 1, 2))
+                s_e(i + 1)
+            flush()
+            if i < 1:
+                lace(2, 0, "SV"[0])
+            if i + 2 < TILES:
+                scores(i + 2)
+            gd_make(i)
+            gd_turn(i)
+            if i + 2 < TILES:
+                te_max(i + 2)
+            flush()
+            if i >= 1:
+                dq_out(i - 1)
+            gd_out(i)
+            if i < 1:
+                widen(2, 1, "SSSS")
+            if 2 <= i < 6:
+                lace_qr((i - 2) // 2, i % 2)
+            if i in (4, 5, 6):
+                gq(0, 4 * (i - 4), 2)
+                gq(0, 4 * (i - 4) + 2, 2)
+            if i < 1:
+                lace(2, 1, "SV"[1])
+                flush()
+            if i + 5 < TILES:
+                load_te(i + 5)
+            if i == 3:
+                load_qr(1)
+        gq(1, 0, 1)
+        flush()
+        gd_q(7)
+        gq(1, 1, 1)
+        flush()
+        dd_pe(0)
+        dq(7)
+        gq(1, 2, 2)
+        flush()
+        dd_out(0, "SV")
+        dd_pe(1)
+        dq_out(7)
+        for c in range(1, 6):
+            if c < 5:
+                gq(1, 2 * c + 2, 2)
+                flush()
+            dd_pe(2 * c)
+            dd_out(2 * c - 1, "SV")
+            dd_pe(2 * c + 1)
+            dd_out(2 * c, "SS")
+        dd_out(11, "SV")

@@ -41,6 +41,7 @@ def tile_crossencoderdistillbiencodergrad_kernel(
         keep = ctx.enter_context(tc.tile_pool(name="keep", bufs=1))
         pool = ctx.enter_context(tc.tile_pool(name="work", bufs=1))
         psum = ctx.enter_context(tc.psum_pool(name="psum", bufs=1))
+        ctx.enter_context(tc.manual_schedule(engines={mybir.EngineType.DVE, mybir.EngineType.Pool}))
 
         ident = keep.tile([P, P], F32, name="ident")
         q_codes = keep.tile([P, TILES, 2, P], U32, name="q_codes", align_bytes=64)
@@ -74,7 +75,7 @@ def tile_crossencoderdistillbiencodergrad_kernel(
         wd_raw = pool.tile([P, ND], BF16, name="wd_raw", tag="gd", bufs=2)
 
         def load_te(i):
-            te_raw[i] = pool.tile([P, ND], BF16, name="te_raw", tag="te", bufs=5)
+            te_raw[i] = pool.tile([P, ND], BF16, name="te_raw", tag="te", bufs=4)
             nc.sync.dma_start(out=te_raw[i][:], in_=te_v[i // PACK, :, i % PACK, :])
 
         def load_dr(s):
@@ -85,11 +86,11 @@ def tile_crossencoderdistillbiencodergrad_kernel(
             nc.sync.dma_start(out=d_raw[:, r : r + n, :], in_=d_v[:, r : r + n, :])
 
         def load_qr(g):
-            qr_raw[g] = pool.tile([P, PACK, D], BF16, name="qr_raw", tag="q8", bufs=3)
+            qr_raw[g] = pool.tile([P, PACK, D], BF16, name="qr_raw", tag="q8", bufs=2)
             nc.sync.dma_start(out=qr_raw[g][:], in_=qr_v[g])
 
         for g in range(GROUPS):
-            q_raw[g] = pool.tile([P, PACK, D], BF16, name="q_raw", tag="q8", bufs=3)
+            q_raw[g] = pool.tile([P, PACK, D], BF16, name="q_raw", tag="q8", bufs=2)
         load_te(0)
         nc.scalar.dma_start(out=drs[:], in_=drs_v)
         load_dr(0)
@@ -106,8 +107,6 @@ def tile_crossencoderdistillbiencodergrad_kernel(
         load_te(2)
         nc.sync.dma_start(out=q_raw[1][:], in_=q_v[1])
         load_te(3)
-        load_te(4)
-        load_qr(0)
 
         nc.gpsimd.memset(dummy[:], 0.0)
         nc.scalar.activation(out=dummy[:, 1:2], in_=dummy[:, 0:1], func=ACT.Exp)
@@ -116,7 +115,7 @@ def tile_crossencoderdistillbiencodergrad_kernel(
         def quantize(codes, scales, grouped):
             nc.vector.quantize_mx(out=codes.bitcast(FP8X4), scales=scales, in_=grouped)
 
-        banks = (("tp", 2), ("o", 3), ("s", 3))
+        banks = (("o", 3), ("tp", 2), ("o", 3))
         count = [0]
 
         def transpose_bank():
@@ -187,7 +186,7 @@ def tile_crossencoderdistillbiencodergrad_kernel(
 
         def widen(s, h, engines="SSSS"):
             cols = slice(512 * h, 512 * (h + 1))
-            wide = pool.tile([P, PACK, 512], BF16, name="wide", tag="wide", bufs=2, align_bytes=64)
+            wide = pool.tile([P, PACK, 512], BF16, name="wide", tag="wide", bufs=3, align_bytes=64)
             for t in range(PACK):
                 if engines[t] == "S":
                     nc.scalar.activation(
@@ -201,23 +200,48 @@ def tile_crossencoderdistillbiencodergrad_kernel(
                     )
             wides[s, h] = wide
 
+        def lace_tile(wide, codes, scales, eng):
+            if eng == "G":
+                grp = pool.tile([P, 512, PACK], BF16, name="ggrp", tag="ggrp", bufs=1, align_bytes=64)
+                nc.gpsimd.tensor_scalar(
+                    out=grp[:], in0=wide.rearrange("p t c -> p c t"), scalar1=1.0, scalar2=0.0,
+                    op0=ALU.mult, op1=ALU.add,
+                )
+            else:
+                grp = pool.tile([P, 512, PACK], BF16, name="rgrp", tag="rgrp", bufs=2, align_bytes=64)
+                copy_out(
+                    eng, grp[:].rearrange("p (c i) t -> p c t i", i=4), wide.rearrange("p t (c i) -> p c t i", i=4)
+                )
+            later.append((codes, scales, grp[:].rearrange("p c t -> p (c t)")))
+
         def lace(s, h, eng="V"):
             cols = slice(512 * h, 512 * (h + 1))
-            grp = pool.tile([P, 512, PACK], BF16, name="rgrp", tag="rgrp", bufs=2, align_bytes=64)
-            copy_out(
-                eng, grp[:].rearrange("p (c i) t -> p c t i", i=4),
-                wides.pop((s, h))[:].rearrange("p t (c i) -> p c t i", i=4),
-            )
-            later.append((dr_codes[:, s, cols], dr_scales[:, s, cols], grp[:].rearrange("p c t -> p (c t)")))
+            lace_tile(wides.pop((s, h))[:], dr_codes[:, s, cols], dr_scales[:, s, cols], eng)
 
-        def lace_qr(g, h, eng="S"):
-            cols = slice(512 * h, 512 * (h + 1))
-            grp = pool.tile([P, 512, PACK], BF16, name="rgrp", tag="rgrp", bufs=2, align_bytes=64)
+        def gq_scale(g, c):
+            cols = slice(512 * c, 512 * (c + 1))
+            wide = pool.tile([P, PACK, 512], BF16, name="wide", tag="wide", bufs=3, align_bytes=64)
+            for t in range(PACK):
+                i = PACK * g + t
+                nc.scalar.activation(out=wide[:, t, :], in_=es[g][:, t, cols], func=ACT.Copy, scale=cwq[:, i : i + 1])
+            wides["g", g, c] = wide
+
+        def gq_lace(g, c, eng):
+            cols = slice(512 * c, 512 * (c + 1))
+            lace_tile(wides.pop(("g", g, c))[:], gq_codes[:, g, cols], gq_scales[:, g, cols], eng)
+
+        def lace_qr(g, k, eng):
+            cols = slice(256 * k, 256 * (k + 1))
+            grp = pool.tile([P, 256, PACK], BF16, name="agrp", tag="agrp", bufs=4, align_bytes=64)
             copy_out(
                 eng, grp[:].rearrange("p (c i) t -> p c t i", i=4),
                 qr_raw[g][:, :, cols].rearrange("p t (c i) -> p c t i", i=4),
             )
             later.append((qr_codes[:, g, cols], qr_scales[:, g, cols], grp[:].rearrange("p c t -> p (c t)")))
+
+        def lace_qr2(g, h, eng):
+            cols = slice(512 * h, 512 * (h + 1))
+            lace_tile(qr_raw[g][:, :, cols], qr_codes[:, g, cols], qr_scales[:, g, cols], eng)
 
         te_exp, es, gds, gd_grp, gdT, obanks = {}, {}, {}, {}, {}, {}
 
@@ -308,8 +332,8 @@ def tile_crossencoderdistillbiencodergrad_kernel(
                 copy_out(e, grp_w[:, k : k + n], sb[i, "g", k][:, 0:n].rearrange("p s u c -> p s c u"))
 
         def gd_q(i):
-            codes = pool.tile([P, 3 * P], U32, name="gdc", tag="gdc", bufs=2, align_bytes=64)
-            scales = pool.tile([P, 3 * P], U8, name="gds", tag="gds", bufs=2, align_bytes=64)
+            codes = pool.tile([P, 3 * P], U32, name="gdc", tag="gdc", bufs=4, align_bytes=64)
+            scales = pool.tile([P, 3 * P], U8, name="gds", tag="gds", bufs=4, align_bytes=64)
             flat = gd_grp[i][:].rearrange("p c e -> p (c e)")
             quantize(codes[:, 0:256], scales[:, 0:256], flat[:, 0:1024])
             quantize(codes[:, 256:384], scales[:, 256:384], flat[:, 1024:1536])
@@ -376,32 +400,33 @@ def tile_crossencoderdistillbiencodergrad_kernel(
 
         te_max(0)
         te_e(0)
+        widen(0, 0, "VVVV")
         q_turn(0)
         q_out(0, "S")
         prep_d(0)
         d_out(0, "SS")
-        widen(0, 0, "SSVV")
-        flush()
+        lace(0, 0, "V")
         prep_d(1)
-        lace(0, 0, "VV"[0])
+        flush(3)
+        widen(0, 1, "SSVV")
         d_out(1, "SS")
-        widen(0, 1, "SSSV")
         flush(1)
-        prep_d(2)
-        flush(2)
-        scores(0, (0,))
-        d_out(2, "SS")
-        lace(0, 1, "VV"[1])
-        load_dr(2)
-        prep_d(3)
-        s_max(0, (0,))
-        flush()
-        d_out(3, "SS")
-        prep_d(4)
         te_max(1)
         flush()
+        prep_d(2)
+        lace(0, 1, "V")
+        scores(0, (0,))
+        d_out(2, "SS")
+        prep_d(3)
+        flush(1)
+        s_max(0, (0,))
+        flush()
+        load_dr(2)
+        d_out(3, "SS")
+        prep_d(4)
+        flush()
         scores(0, (1,))
-        d_out(4, "SS")
+        d_out(4, "SV")
         prep_d(5)
         s_max(0, (1,))
         q_turn(1)
@@ -413,82 +438,87 @@ def tile_crossencoderdistillbiencodergrad_kernel(
         nc.gpsimd.tensor_scalar(
             out=wd_big[:], in0=wd_raw[:], scalar1=float(ND), scalar2=0.0, op0=ALU.mult, op1=ALU.add
         )
+        widen(1, 0, "SSSS")
         d_out(5, "SV")
         q_out(1, "S")
         flush()
         scores(0, (2,))
         scores(1)
         q_turn(2)
+        lace(1, 0, "V")
+        widen(1, 1, "SSSS")
+        q_out(2, "S")
         s_max(0, (2,))
         s_e(0)
-        q_out(2, "S")
-        for h in range(2):
-            widen(1, h, "SSSS")
-            lace(1, h, "SS"[h])
+        widen(2, 0, "SSSS")
+        flush()
+        lace(1, 1, "V")
+        te_e(1)
+        flush()
         for i in range(TILES):
-            if i == 0:
-                s_max(1, (0,))
             stats(i)
             if i + 3 < TILES:
                 q_turn(i + 3)
+            if i == 0:
+                load_qr(0)
+            if i == 4:
+                load_qr(1)
             h_make(i)
-            if i + 1 < TILES:
-                te_e(i + 1)
-            if i + 3 < TILES:
-                q_out(i + 3, "S")
             if i >= 1:
-                gd_q(i - 1)
-                dq(i - 1)
-            if i < 1:
-                widen(2, 0, "SSSS")
-            if i + 1 < TILES:
-                s_max(i + 1, (1, 2) if i == 0 else (0, 1, 2))
-                s_e(i + 1)
+                gd_out(i - 1)
             flush()
-            if i < 1:
-                lace(2, 0, "SV"[0])
+            if i < 2:
+                lace(2, i, "G")
+            elif i < 4:
+                lace_qr2(0, i - 2, "G")
+            elif i < 7:
+                gq_scale(0, i - 4)
+                gq_lace(0, i - 4, "G")
+            if i + 1 < TILES:
+                s_max(i + 1)
+                s_e(i + 1)
             if i + 2 < TILES:
                 scores(i + 2)
+                te_max(i + 2)
+                te_e(i + 2)
+            if i >= 1:
+                gd_q(i - 1)
+            if i == 2:
+                dq(0)
+            if i >= 2:
+                dq(i - 1)
+            if i + 3 < TILES:
+                q_out(i + 3, "S")
+            if i == 0:
+                widen(2, 1, "SSSS")
+            if i == 7:
+                gq(1, 0, 2)
+                flush()
             gd_make(i)
             gd_turn(i)
-            if i + 2 < TILES:
-                te_max(i + 2)
-            flush()
-            if i >= 1:
+            if i == 2:
+                dq_out(0)
+            if i >= 2:
                 dq_out(i - 1)
-            gd_out(i)
-            if i < 1:
-                widen(2, 1, "SSSS")
-            if 2 <= i < 6:
-                lace_qr((i - 2) // 2, i % 2)
-            if i in (4, 5, 6):
-                gq(0, 4 * (i - 4), 2)
-                gq(0, 4 * (i - 4) + 2, 2)
-            if i < 1:
-                lace(2, 1, "SV"[1])
+            if i in (5, 6):
+                lace_qr(1, 2 * (i - 5), "S")
+                lace_qr(1, 2 * (i - 5) + 1, "S")
+            if i + 4 < TILES:
+                load_te(i + 4)
+        dd_eng = ["SS","SS","SV","SS","SS","SV","SS","SS","SV","SV","SV","SV"]
+        for c in range(6):
+            if c == 2:
+                gd_out(7)
+                gd_q(7)
+            if c > 0:
+                gq(1, 2 * c, 2)
                 flush()
-            if i + 5 < TILES:
-                load_te(i + 5)
-            if i == 3:
-                load_qr(1)
-        gq(1, 0, 1)
-        flush()
-        gd_q(7)
-        gq(1, 1, 1)
-        flush()
-        dd_pe(0)
-        dq(7)
-        gq(1, 2, 2)
-        flush()
-        dd_out(0, "SV")
-        dd_pe(1)
-        dq_out(7)
-        for c in range(1, 6):
-            if c < 5:
-                gq(1, 2 * c + 2, 2)
-                flush()
+            if c == 3:
+                dq(7)
+                dq_out(7)
             dd_pe(2 * c)
-            dd_out(2 * c - 1, "SV")
+            if c > 0:
+                dd_out(2 * c - 1, dd_eng[2 * c - 1])
             dd_pe(2 * c + 1)
-            dd_out(2 * c, "SS")
-        dd_out(11, "SV")
+            dd_out(2 * c, dd_eng[2 * c])
+        dd_out(11, dd_eng[11])

from contextlib import ExitStack

import concourse.mybir as mybir
from concourse.masks import make_identity

NQ, ND, D = 1024, 1536, 1024
FLOPS = 3 * 2 * NQ * ND * D

F32 = mybir.dt.float32
BF16 = mybir.dt.bfloat16
U32 = mybir.dt.uint32
U8 = mybir.dt.uint8
FP8 = mybir.dt.float8_e4m3fn
FP8X4 = mybir.dt.float8_e4m3fn_x4
ALU = mybir.AluOpType
ACT = mybir.ActivationFunctionType

P = 128
PACK = 4
GROUPS = 2
TILES = 8
SCALE = 1.0 / 32.0


def tile_crossencoderdistillbiencodergrad_kernel(
    tc, q, d, teacher, dr_bytes, dr_scale, qr, wd, wq, out_0, out_1
):
    nc = tc.nc

    q_v = q.rearrange("(g p t) k -> g p t k", p=P, t=PACK)
    d_v = d.rearrange("(r p) k -> p r k", p=P)
    te_v = teacher.rearrange("(g p t) n -> g p t n", p=P, t=PACK)
    drb_v = dr_bytes.rearrange("(s p t) n -> s p t n", p=P, t=PACK)
    drs_v = dr_scale.rearrange("(s p t) o -> p s (t o)", p=P, t=PACK)
    qr_v = qr.rearrange("(g p t) n -> g p t n", p=P, t=PACK)
    wq_v = wq.rearrange("(g p t) -> p g t", p=P, t=PACK)
    dq_v = out_0.rearrange("(g p t) n -> g t p n", p=P, t=PACK)
    dd_v = out_1.rearrange("(j p) n -> j p n", p=P)

    with ExitStack() as ctx:
        keep = ctx.enter_context(tc.tile_pool(name="keep", bufs=1))
        pool = ctx.enter_context(tc.tile_pool(name="work", bufs=1))
        psum = ctx.enter_context(tc.psum_pool(name="psum", bufs=1))
        ctx.enter_context(tc.manual_schedule(engines={mybir.EngineType.DVE, mybir.EngineType.Pool}))

        ident = keep.tile([P, P], F32, name="ident")
        q_codes = keep.tile([P, TILES, 2, P], U32, name="q_codes", align_bytes=64)
        q_scales = keep.tile([P, TILES, 2, P], U8, name="q_scales", align_bytes=64)
        d_codes = keep.tile([P, 2, ND], U32, name="d_codes", align_bytes=64)
        d_scales = keep.tile([P, 2, ND], U8, name="d_scales", align_bytes=64)
        dr_codes = keep.tile([P, 3, D], U32, name="dr_codes", align_bytes=64)
        dr_scales = keep.tile([P, 3, D], U8, name="dr_scales", align_bytes=64)
        qr_codes = keep.tile([P, 2, D], U32, name="qr_codes", align_bytes=64)
        qr_scales = keep.tile([P, 2, D], U8, name="qr_scales", align_bytes=64)
        gq_codes = keep.tile([P, 2, ND], U32, name="gq_codes", align_bytes=64)
        gq_scales = keep.tile([P, 2, ND], U8, name="gq_scales", align_bytes=64)

        drs = keep.tile([P, 3, PACK], F32, name="drs")
        wq_raw = keep.tile([P, GROUPS, PACK], BF16, name="wq_raw")
        wq_big = keep.tile([P, TILES], F32, name="wq_big")
        wd_big = keep.tile([P, ND], F32, name="wd_big")
        cwq = keep.tile([P, TILES], F32, name="cwq")
        s_min = keep.tile([P, TILES, 4], F32, name="s_min")
        s_neg = keep.tile([P, TILES], F32, name="s_neg")
        t_neg = keep.tile([P, TILES], F32, name="t_neg")
        s_sum = keep.tile([P, TILES], F32, name="s_sum")
        t_sum = keep.tile([P, TILES], F32, name="t_sum")
        t_rec = keep.tile([P, TILES], F32, name="t_rec")
        s_rec = keep.tile([P, TILES], F32, name="s_rec")
        ratio = keep.tile([P, TILES], F32, name="ratio")
        dummy = keep.tile([P, 2], F32, name="dummy")

        q_raw, dr_raw, te_raw, qr_raw = {}, {}, {}, {}
        d_raw = pool.tile([P, 12, D], BF16, name="d_raw", tag="big", bufs=2)
        wd_raw = pool.tile([P, ND], BF16, name="wd_raw", tag="gd", bufs=2)

        def load_te(i):
            te_raw[i] = pool.tile([P, ND], BF16, name="te_raw", tag="te", bufs=4)
            nc.sync.dma_start(out=te_raw[i][:], in_=te_v[i // PACK, :, i % PACK, :])

        def load_dr(s):
            dr_raw[s] = pool.tile([P, PACK, D], U8, name="dr_raw", tag="drb", bufs=2)
            nc.sync.dma_start(out=dr_raw[s][:], in_=drb_v[s])

        def load_d(r, n):
            nc.sync.dma_start(out=d_raw[:, r : r + n, :], in_=d_v[:, r : r + n, :])

        def load_qr(g):
            qr_raw[g] = pool.tile([P, PACK, D], BF16, name="qr_raw", tag="q8", bufs=2)
            nc.sync.dma_start(out=qr_raw[g][:], in_=qr_v[g])

        for g in range(GROUPS):
            q_raw[g] = pool.tile([P, PACK, D], BF16, name="q_raw", tag="q8", bufs=2)
        load_te(0)
        nc.scalar.dma_start(out=drs[:], in_=drs_v)
        load_dr(0)
        nc.sync.dma_start(out=q_raw[0][:, 0, :], in_=q_v[0, :, 0, :])
        for r in range(0, 4, 2):
            load_d(r, 2)
        load_te(1)
        for r in range(4, 12, 2):
            load_d(r, 2)
        nc.sync.dma_start(out=q_raw[0][:, 1:4, :], in_=q_v[0, :, 1:4, :])
        nc.sync.dma_start(out=wq_raw[:], in_=wq_v)
        nc.sync.dma_start(out=wd_raw[:], in_=wd.partition_broadcast(P))
        load_dr(1)
        load_te(2)
        nc.sync.dma_start(out=q_raw[1][:], in_=q_v[1])
        load_te(3)

        nc.gpsimd.memset(dummy[:], 0.0)
        nc.scalar.activation(out=dummy[:, 1:2], in_=dummy[:, 0:1], func=ACT.Exp)
        make_identity(nc, ident[:])

        def quantize(codes, scales, grouped):
            nc.vector.quantize_mx(out=codes.bitcast(FP8X4), scales=scales, in_=grouped)

        banks = (("o", 3), ("tp", 2), ("o", 3))
        count = [0]

        def transpose_bank():
            tag, bufs = banks[count[0] % 3]
            count[0] += 1
            return psum.tile([P, 2, 2, P], F32, name="tbank", tag=tag, bufs=bufs)

        def copy_out(eng, out, in_):
            if eng == "V":
                nc.vector.tensor_copy(out=out, in_=in_)
            else:
                nc.scalar.copy(out=out, in_=in_)

        def as_words(grp):
            return grp[:].rearrange("p c e -> p (c e)").bitcast(F32)

        sb = {}
        later = []

        def prep_d(rr):
            for s in range(2):
                bank = transpose_bank()
                for j in range(2):
                    words = d_raw[:, 2 * rr + j, :].bitcast(F32)
                    for u in range(2):
                        nc.tensor.transpose(bank[:, j, u, :], words[:, 256 * s + u : 256 * (s + 1) : 2], ident[:])
                sb["d", rr, s] = bank

        def d_out(rr, engines):
            for s in range(2):
                grp = pool.tile([P, 256, PACK], BF16, name="agrp", tag="agrp", bufs=4, align_bytes=64)
                copy_out(
                    engines[s], as_words(grp).rearrange("p (j c u) -> p j c u", j=2, u=2),
                    sb["d", rr, s][:].rearrange("p j u c -> p j c u"),
                )
                cols = slice(256 * rr, 256 * (rr + 1))
                later.append((d_codes[:, s, cols], d_scales[:, s, cols], grp[:].rearrange("p c e -> p (c e)")))

        def flush(n=99):
            for k in range(min(n, len(later))):
                quantize(*later.pop(0))

        def prep_q(i, eng):
            q_turn(i)
            q_out(i, eng)

        def q_turn(i):
            words = q_raw[i // PACK][:, i % PACK, :].bitcast(F32)
            bank = transpose_bank() if i == 0 else psum.tile([P, 2, 2, P], F32, name="tbank", tag="tp", bufs=2)
            for s in range(2):
                for u in range(2):
                    nc.tensor.transpose(bank[:, s, u, :], words[:, 256 * s + u : 256 * (s + 1) : 2], ident[:])
            sb["q", i] = bank

        def q_out(i, eng):
            bank = sb["q", i]
            grp = pool.tile([P, 256, PACK], BF16, name="agrp", tag="agrp", bufs=4, align_bytes=64)
            copy_out(
                eng, as_words(grp).rearrange("p (j c u) -> p j c u", j=2, u=2),
                bank[:].rearrange("p j u c -> p j c u"),
            )
            later.append((
                q_codes[:, i].rearrange("p s c -> p (s c)"), q_scales[:, i].rearrange("p s c -> p (s c)"),
                grp[:].rearrange("p c e -> p (c e)"),
            ))

        wides = {}

        def widen(s, h, engines="SSSS"):
            cols = slice(512 * h, 512 * (h + 1))
            wide = pool.tile([P, PACK, 512], BF16, name="wide", tag="wide", bufs=3, align_bytes=64)
            for t in range(PACK):
                if engines[t] == "S":
                    nc.scalar.activation(
                        out=wide[:, t, :], in_=dr_raw[s][:, t, cols].bitcast(FP8), func=ACT.Copy,
                        scale=drs[:, s, t : t + 1],
                    )
                else:
                    nc.vector.tensor_scalar(
                        out=wide[:, t, :], in0=dr_raw[s][:, t, cols].bitcast(FP8), scalar1=drs[:, s, t : t + 1],
                        scalar2=None, op0=ALU.mult,
                    )
            wides[s, h] = wide

        def lace_tile(wide, codes, scales, eng):
            if eng == "G":
                grp = pool.tile([P, 512, PACK], BF16, name="ggrp", tag="ggrp", bufs=1, align_bytes=64)
                nc.gpsimd.tensor_scalar(
                    out=grp[:], in0=wide.rearrange("p t c -> p c t"), scalar1=1.0, scalar2=0.0,
                    op0=ALU.mult, op1=ALU.add,
                )
            else:
                grp = pool.tile([P, 512, PACK], BF16, name="rgrp", tag="rgrp", bufs=2, align_bytes=64)
                copy_out(
                    eng, grp[:].rearrange("p (c i) t -> p c t i", i=4), wide.rearrange("p t (c i) -> p c t i", i=4)
                )
            later.append((codes, scales, grp[:].rearrange("p c t -> p (c t)")))

        def lace(s, h, eng="V"):
            cols = slice(512 * h, 512 * (h + 1))
            lace_tile(wides.pop((s, h))[:], dr_codes[:, s, cols], dr_scales[:, s, cols], eng)

        def gq_scale(g, c):
            cols = slice(512 * c, 512 * (c + 1))
            wide = pool.tile([P, PACK, 512], BF16, name="wide", tag="wide", bufs=3, align_bytes=64)
            for t in range(PACK):
                i = PACK * g + t
                nc.scalar.activation(out=wide[:, t, :], in_=es[g][:, t, cols], func=ACT.Copy, scale=cwq[:, i : i + 1])
            wides["g", g, c] = wide

        def gq_lace(g, c, eng):
            cols = slice(512 * c, 512 * (c + 1))
            lace_tile(wides.pop(("g", g, c))[:], gq_codes[:, g, cols], gq_scales[:, g, cols], eng)

        def lace_qr(g, k, eng):
            cols = slice(256 * k, 256 * (k + 1))
            grp = pool.tile([P, 256, PACK], BF16, name="agrp", tag="agrp", bufs=4, align_bytes=64)
            copy_out(
                eng, grp[:].rearrange("p (c i) t -> p c t i", i=4),
                qr_raw[g][:, :, cols].rearrange("p t (c i) -> p c t i", i=4),
            )
            later.append((qr_codes[:, g, cols], qr_scales[:, g, cols], grp[:].rearrange("p c t -> p (c t)")))

        def lace_qr2(g, h, eng):
            cols = slice(512 * h, 512 * (h + 1))
            lace_tile(qr_raw[g][:, :, cols], qr_codes[:, g, cols], qr_scales[:, g, cols], eng)

        te_exp, es, gds, gd_grp, gdT, obanks = {}, {}, {}, {}, {}, {}

        def te_max(i):
            nc.vector.tensor_scalar(
                out=te_raw[i][:], in0=te_raw[i][:], scalar1=-1.0, scalar2=None, op0=ALU.mult, op1=ALU.min,
                accum_out=t_neg[:, i : i + 1],
            )

        def te_e(i):
            te_exp[i] = pool.tile([P, ND], F32, name="te_exp", tag="te_exp", bufs=2)
            nc.scalar.activation(
                out=te_exp[i][:], in_=te_raw[i][:], func=ACT.Exp, scale=-1.0, bias=t_neg[:, i : i + 1],
                accum_out=t_sum[:, i : i + 1],
            )

        def scores(i, chunks=(0, 1, 2)):
            for n in chunks:
                cols = slice(512 * n, 512 * (n + 1))
                sb[i, n] = psum.tile([P, 512], F32, name="sbank", tag="s", bufs=3)
                for s in range(2):
                    nc.tensor.matmul_mx(
                        out=sb[i, n][:],
                        lhsT=q_codes[:, i, s, :].bitcast(FP8X4), lhsT_scale=q_scales[:, i, s, :],
                        rhs=d_codes[:, s, cols].bitcast(FP8X4), rhs_scale=d_scales[:, s, cols],
                        start=(s == 0), stop=(s == 1),
                    )

        def s_max(i, chunks=(0, 1, 2)):
            g, t = i // PACK, i % PACK
            if g not in es:
                es[g] = pool.tile([P, PACK, ND], F32, name="es", tag="big", bufs=2)
            for n in chunks:
                cols = slice(512 * n, 512 * (n + 1))
                nc.vector.tensor_scalar(
                    out=es[g][:, t, cols], in0=sb[i, n][:], scalar1=-SCALE, scalar2=None, op0=ALU.mult, op1=ALU.min,
                    accum_out=s_min[:, i, n : n + 1],
                )
            if 2 not in chunks:
                return
            nc.vector.tensor_reduce(
                out=s_neg[:, i : i + 1], in_=s_min[:, i, 0:3], op=ALU.min, axis=mybir.AxisListType.X
            )

        def s_e(i):
            e = es[i // PACK][:, i % PACK, :]
            nc.scalar.activation(
                out=e, in_=e, func=ACT.Exp, scale=-1.0, bias=s_neg[:, i : i + 1], accum_out=s_sum[:, i : i + 1]
            )

        def stats(i):
            nc.vector.reciprocal(out=t_rec[:, i : i + 1], in_=t_sum[:, i : i + 1])
            nc.vector.reciprocal(out=s_rec[:, i : i + 1], in_=s_sum[:, i : i + 1])
            nc.vector.tensor_scalar(
                out=ratio[:, i : i + 1], in0=s_sum[:, i : i + 1], scalar1=t_rec[:, i : i + 1], scalar2=-1.0,
                op0=ALU.mult, op1=ALU.mult,
            )
            nc.gpsimd.tensor_tensor(
                out=cwq[:, i : i + 1], in0=s_rec[:, i : i + 1], in1=wq_big[:, i : i + 1], op=ALU.mult
            )

        def h_make(i):
            h = es[i // PACK][:, i % PACK, :]
            nc.vector.scalar_tensor_tensor(
                out=h, in0=te_exp[i][:], scalar=ratio[:, i : i + 1], in1=h, op0=ALU.mult, op1=ALU.add
            )

        def gd_make(i):
            gds[i] = pool.tile([P, ND], BF16, name="gd", tag="gd", bufs=2)
            nc.vector.scalar_tensor_tensor(
                out=gds[i][:], in0=es[i // PACK][:, i % PACK, :], scalar=s_rec[:, i : i + 1], in1=wd_big[:],
                op0=ALU.mult, op1=ALU.mult,
            )

        def gd_turn(i):
            words = gds[i][:].bitcast(F32)
            for k, n in ((0, 2), (2, 1)):
                bank = psum.tile([P, 2, 2, P], F32, name="gbank", tag="tp", bufs=2)
                for s in range(k, k + n):
                    for u in range(2):
                        nc.tensor.transpose(bank[:, s - k, u, :], words[:, 256 * s + u : 256 * (s + 1) : 2], ident[:])
                sb[i, "g", k] = bank

        def gd_out(i, engines="SS"):
            gd_grp[i] = pool.tile([P, 3 * P, PACK], BF16, name="gdgrp", tag="gdgrp", bufs=2, align_bytes=64)
            grp_w = as_words(gd_grp[i]).rearrange("p (s c u) -> p s c u", s=3, u=2)
            for e, (k, n) in zip(engines, ((0, 2), (2, 1))):
                copy_out(e, grp_w[:, k : k + n], sb[i, "g", k][:, 0:n].rearrange("p s u c -> p s c u"))

        def gd_q(i):
            codes = pool.tile([P, 3 * P], U32, name="gdc", tag="gdc", bufs=4, align_bytes=64)
            scales = pool.tile([P, 3 * P], U8, name="gds", tag="gds", bufs=4, align_bytes=64)
            flat = gd_grp[i][:].rearrange("p c e -> p (c e)")
            quantize(codes[:, 0:256], scales[:, 0:256], flat[:, 0:1024])
            quantize(codes[:, 256:384], scales[:, 256:384], flat[:, 1024:1536])
            gdT[i] = (codes, scales)

        def dq(i):
            codes, scales = gdT[i]
            for h in range(2):
                cols = slice(512 * h, 512 * (h + 1))
                obanks[i, h] = psum.tile([P, 512], F32, name="obank", tag="o", bufs=3)
                for s in range(3):
                    k = slice(P * s, P * (s + 1))
                    nc.tensor.matmul_mx(
                        out=obanks[i, h][:],
                        lhsT=codes[:, k].bitcast(FP8X4), lhsT_scale=scales[:, k],
                        rhs=dr_codes[:, s, cols].bitcast(FP8X4), rhs_scale=dr_scales[:, s, cols],
                        start=(s == 0), stop=(s == 2),
                    )

        def dq_out(i, engines="SS"):
            res = pool.tile([P, D], F32, name="res", tag="res", bufs=3)
            for h in range(2):
                copy_out(engines[h], res[:, 512 * h : 512 * (h + 1)], obanks[i, h][:])
            nc.sync.dma_start(out=dq_v[i // PACK, i % PACK], in_=res[:])

        def gq(g, a, n):
            cols = slice(128 * a, 128 * (a + n))
            grp = pool.tile([P, 256, PACK], BF16, name="qgrp", tag="agrp", bufs=4, align_bytes=64)
            gain = cwq[:, PACK * g : PACK * (g + 1)].unsqueeze(1).unsqueeze(3).to_broadcast([P, 32 * n, PACK, 4])
            nc.vector.tensor_tensor(
                out=grp[:, 0 : 128 * n].rearrange("p (c i) t -> p c t i", i=4),
                in0=es[g][:, :, cols].rearrange("p t (c i) -> p c t i", i=4),
                in1=gain, op=ALU.mult,
            )
            later.append((gq_codes[:, g, cols], gq_scales[:, g, cols], grp[:, 0 : 128 * n].rearrange("p c t -> p (c t)")))

        dd_banks = (("o", 3), ("s", 3), ("tp", 2))
        dd_count = [0]

        def dd_pe(j):
            k = slice(P * j, P * (j + 1))
            for h in range(2):
                cols = slice(512 * h, 512 * (h + 1))
                tag, bufs = dd_banks[dd_count[0] % 3]
                dd_count[0] += 1
                bank = psum.tile([P, 512], F32, name="dbank", tag=tag, bufs=bufs)
                for g in range(GROUPS):
                    nc.tensor.matmul_mx(
                        out=bank[:],
                        lhsT=gq_codes[:, g, k].bitcast(FP8X4), lhsT_scale=gq_scales[:, g, k],
                        rhs=qr_codes[:, g, cols].bitcast(FP8X4), rhs_scale=qr_scales[:, g, cols],
                        start=(g == 0), stop=(g == 1),
                    )
                obanks["d", j, h] = bank

        def dd_out(j, engines):
            if j % 5 < 3:
                res = pool.tile([P, D], F32, name="res", tag="res", bufs=3)
            else:
                res = pool.tile([P, D], F32, name="res2", tag="te_exp", bufs=2)
            for h in range(2):
                copy_out(engines[h], res[:, 512 * h : 512 * (h + 1)], obanks["d", j, h][:])
            nc.sync.dma_start(out=dd_v[j], in_=res[:])

        te_max(0)
        te_e(0)
        widen(0, 0, "VVVV")
        q_turn(0)
        q_out(0, "S")
        prep_d(0)
        d_out(0, "SS")
        lace(0, 0, "V")
        prep_d(1)
        flush(3)
        widen(0, 1, "SSVV")
        d_out(1, "SS")
        flush(1)
        te_max(1)
        flush()
        prep_d(2)
        lace(0, 1, "V")
        scores(0, (0,))
        d_out(2, "SS")
        prep_d(3)
        flush(1)
        s_max(0, (0,))
        flush()
        load_dr(2)
        d_out(3, "SS")
        prep_d(4)
        flush()
        scores(0, (1,))
        d_out(4, "SV")
        prep_d(5)
        s_max(0, (1,))
        q_turn(1)
        flush()
        nc.gpsimd.tensor_scalar(
            out=wq_big[:], in0=wq_raw[:].rearrange("p g t -> p (g t)"), scalar1=float(ND), scalar2=0.0,
            op0=ALU.mult, op1=ALU.add,
        )
        nc.gpsimd.tensor_scalar(
            out=wd_big[:], in0=wd_raw[:], scalar1=float(ND), scalar2=0.0, op0=ALU.mult, op1=ALU.add
        )
        widen(1, 0, "SSSS")
        d_out(5, "SV")
        q_out(1, "S")
        flush()
        scores(0, (2,))
        scores(1)
        q_turn(2)
        lace(1, 0, "V")
        widen(1, 1, "SSSS")
        q_out(2, "S")
        s_max(0, (2,))
        s_e(0)
        widen(2, 0, "SSSS")
        flush()
        lace(1, 1, "V")
        te_e(1)
        flush()
        for i in range(TILES):
            stats(i)
            if i + 3 < TILES:
                q_turn(i + 3)
            if i == 0:
                load_qr(0)
            if i == 4:
                load_qr(1)
            h_make(i)
            if i >= 1:
                gd_out(i - 1)
            flush()
            if i < 2:
                lace(2, i, "G")
            elif i < 4:
                lace_qr2(0, i - 2, "G")
            elif i < 7:
                gq_scale(0, i - 4)
                gq_lace(0, i - 4, "G")
            if i + 1 < TILES:
                s_max(i + 1)
                s_e(i + 1)
            if i + 2 < TILES:
                scores(i + 2)
                te_max(i + 2)
                te_e(i + 2)
            if i >= 1:
                gd_q(i - 1)
            if i == 2:
                dq(0)
            if i >= 2:
                dq(i - 1)
            if i + 3 < TILES:
                q_out(i + 3, "S")
            if i == 0:
                widen(2, 1, "SSSS")
            if i == 7:
                gq(1, 0, 2)
                flush()
            gd_make(i)
            gd_turn(i)
            if i == 2:
                dq_out(0)
            if i >= 2:
                dq_out(i - 1)
            if i in (5, 6):
                lace_qr(1, 2 * (i - 5), "S")
                lace_qr(1, 2 * (i - 5) + 1, "S")
            if i + 4 < TILES:
                load_te(i + 4)
        dd_eng = ["SS","SS","SV","SS","SS","SV","SS","SS","SV","SV","SV","SV"]
        for c in range(6):
            if c == 2:
                gd_out(7)
                gd_q(7)
            if c > 0:
                gq(1, 2 * c, 2)
                flush()
            if c == 3:
                dq(7)
                dq_out(7)
            dd_pe(2 * c)
            if c > 0:
                dd_out(2 * c - 1, dd_eng[2 * c - 1])
            dd_pe(2 * c + 1)
            dd_out(2 * c, dd_eng[2 * c])
        dd_out(11, dd_eng[11])
